import numpy as np
import ml_dtypes


def mxq(x, axis, fmt="e4m3"):
    dtype, down = {"e4m3": (ml_dtypes.float8_e4m3fn, 7), "e5m2": (ml_dtypes.float8_e5m2, 14)}[fmt]
    v = np.moveaxis(np.asarray(x, np.float32).astype(ml_dtypes.bfloat16).astype(np.float64), axis, -1)
    blocks = v.reshape(v.shape[:-1] + (-1, 32))
    amax = np.abs(blocks).max(-1, keepdims=True)
    byte = np.maximum(np.where(amax > 0, np.frexp(amax)[1] - 1 + 127, 0) - down, 1)
    scale = np.exp2(byte - 127.0)
    codes = (blocks / scale).astype(np.float32).astype(dtype).astype(np.float64)
    return np.moveaxis((codes * scale).reshape(v.shape), -1, axis)


WIDE = False


def mx_kscale(k):
    if not WIDE:
        return np.ones(k)
    levels = np.array([10, -10, 5, -5, 0])
    if k % 512:
        return np.exp2(np.random.permutation(np.resize(levels, k // 32))).repeat(32)
    a = np.empty((k // 512, 16))
    for p in range(k // 512):
        a[p, :8] = np.random.permutation(np.resize(levels, 8))
        for g in range(8):
            far = levels[np.abs(levels - a[p, g]) >= 10]
            a[p, g + 8] = far[np.random.randint(len(far))]
    return np.exp2(a.ravel()).repeat(32)


def f64(x):
    return np.asarray(x).astype(np.float64)


def striped(idx):
    return np.tile(np.asarray(idx).reshape(-1, 16).T, (8, 1)).astype(np.uint16)


def unstriped(offs):
    return offs[:16].T.reshape(-1).astype(np.int64)


E2M1 = np.array([0.0, 0.5, 1.0, 1.5, 2.0, 3.0, 4.0, 6.0, -0.0, -0.5, -1.0, -1.5, -2.0, -3.0, -4.0, -6.0])


def pack_weight(w, fmt):
    k, n = w.shape
    w = f64(np.asarray(w, np.float32).astype(ml_dtypes.bfloat16)).reshape(k // 32, 32, n)
    amax = np.abs(w).max(1)
    if fmt == "e4m3":
        byte = np.frexp(amax)[1] - 1 + 127 - 7
    else:
        mant, ex = np.frexp(amax / 6.0)
        byte = np.where(mant > 0.5, ex, ex - 1) + 127
    byte = np.clip(np.where(amax > 0, byte, 1), 1, 254)
    scaled = (w * np.exp2(127.0 - byte)[:, None, :]).reshape(k, n).astype(np.float32)
    by_word = np.ascontiguousarray(scaled.reshape(k // 512, 128, 4, n).transpose(0, 1, 3, 2))
    if fmt == "e4m3":
        words = by_word.astype(ml_dtypes.float8_e4m3fn).view(np.uint8)
    else:
        c = by_word.astype(ml_dtypes.float4_e2m1fn).view(np.uint8) & 0xF
        words = (c[..., 0::2] | (c[..., 1::2] << 4)).reshape(k // 512, 128, 2 * n)
    return np.ascontiguousarray(words), np.ascontiguousarray(byte.astype(np.uint8).reshape(k // 512, 16, n))


def unpack_weight(words, scales, fmt):
    g, _, n = scales.shape
    words = np.ascontiguousarray(words).reshape(g, 128, n, -1)
    if fmt == "e4m3":
        vals = words.view(ml_dtypes.float8_e4m3fn).astype(np.float64)
    else:
        nib = np.empty((g, 128, n, 4), np.uint8)
        nib[..., 0::2] = words & 0xF
        nib[..., 1::2] = words >> 4
        vals = E2M1[nib]
    vals = vals * np.repeat(np.exp2(scales.astype(np.float64) - 127.0), 8, axis=1)[..., None]
    return vals.transpose(0, 1, 3, 2).reshape(g * 512, n)


K, N, T, J = 1024, 512, 1024, 512


def setup_inputs():
    n = np.random.standard_normal
    idx = np.random.permutation(T)[:J]
    fk = mx_kscale(K)
    xtp = pack_weight(n((K, T)) / fk[:, None], "e4m3")
    return {
        "xt_words": xtp[0],
        "xt_scales": xtp[1],
        "wn": (n((K, N)) * 1 / np.sqrt(K) * fk[:, None]).astype(np.float32),
        "g": (n((N, T))).astype(np.float32),
        "of": (np.random.uniform(-1.0, 1.0, (1, N))).astype(np.float32),
        "rw": (np.random.uniform(0.4, 1.2, (J, 1))).astype(np.float32),
        "offs": striped(idx),
    }


def reference(xt_words, xt_scales, wn, g, of, rw, offs):
    idx = unstriped(offs)
    xtu = unpack_weight(xt_words, xt_scales, "e4m3")
    xtidxg = xtu[:, idx]
    wnq = mxq(f64(wn), 0, "e4m3")
    p = xtidxg.T @ wnq
    a = p + f64(of)
    g0 = f64(g)[:, idx].T
    b = g0 + f64(of)
    y = f64(rw) * (b - a * np.mean(a * b, axis=1, keepdims=True) / (np.mean(np.square(a), axis=1, keepdims=True) + 0.1))
    return y

@@ -1,0 +1,209 @@
+from contextlib import ExitStack
+
+import concourse.mybir as mybir
+from concourse.masks import make_identity
+
+K, N, T, J = 1024, 512, 1024, 512
+FLOPS = 2 * K * N * J
+
+F32 = mybir.dt.float32
+BF16 = mybir.dt.bfloat16
+I32 = mybir.dt.int32
+U32 = mybir.dt.uint32
+U16 = mybir.dt.uint16
+U8 = mybir.dt.uint8
+FP8X4 = mybir.dt.float8_e4m3fn_x4
+ACT = mybir.ActivationFunctionType
+ALU = mybir.AluOpType
+
+P = 128
+HALF = N // 2
+TILES = J // P
+OFFS_PER_TILE = P // 16
+
+
+def tile_moe_gradient_off_expert_answer_kernel(tc, xt_words, xt_scales, wn, g, of, rw, offs, out):
+    nc = tc.nc
+    with ExitStack() as ctx:
+        lists = ctx.enter_context(tc.tile_pool(name="lists", bufs=1))
+        sb = ctx.enter_context(tc.tile_pool(name="sb", bufs=1))
+        ps = ctx.enter_context(tc.psum_pool(name="ps", bufs=1))
+
+        offsets = lists.tile([P, J // 16], U16, name="offsets")
+        x_win = [sb.tile([P, T], I32, name=f"x_win{z}") for z in range(2)]
+        s_win = sb.tile([P, T], U8, name="s_win")
+        g_win = [sb.tile([P, T], F32, name=f"g_win{c}") for c in range(4)]
+        w_raw = {(z, h): sb.tile([P, 4, HALF], F32, name=f"w_raw{z}{h}") for z in range(2) for h in range(2)}
+        w_bf = {(z, h): sb.tile([P, HALF, 4], BF16, name=f"w_bf{z}{h}", align_bytes=64) for z in range(2) for h in range(2)}
+        w_codes = {(z, h): sb.tile([P, HALF], U32, name=f"w_codes{z}{h}", align_bytes=64) for z in range(2) for h in range(2)}
+        w_scales = {(z, h): sb.tile([P, HALF], U8, name=f"w_scales{z}{h}", align_bytes=64) for z in range(2) for h in range(2)}
+        x_codes = [sb.tile([P, J], U32, name=f"x_codes{z}", align_bytes=64) for z in range(2)]
+        x_scales = sb.tile([P, J], U8, name="x_scales", align_bytes=64)
+        g_t = [sb.tile([P, J], F32, name=f"g_t{c}") for c in range(3)]
+        g_last = [sb.tile([P, P], F32, name=f"g_last{t}") for t in range(TILES)]
+        a_t = [sb.tile([P, J], F32, name=f"a_t{c}") for c in range(4)]
+        b_sb = [sb.tile([P, N], F32, name=f"b_sb{t}") for t in range(TILES)]
+        res = [sb.tile([P, N], F32, name=f"res{t}") for t in range(TILES)]
+        scaled = [sb.tile([P, N], F32, name=f"scaled{t}") for t in range(TILES)]
+        ident = sb.tile([P, P], F32, name="ident")
+        of_rows = sb.tile([P, P], F32, name="of_rows")
+        rw_rows = sb.tile([P, P], F32, name="rw_rows")
+        of_col = sb.tile([P, 4], F32, name="of_col")
+        rw_col = sb.tile([P, 4], F32, name="rw_col")
+        stat = {(nm, t): sb.tile([P, 1], F32, name=f"{nm}{t}") for nm in ("aa", "ab", "den", "inv", "coef") for t in range(TILES)}
+
+        b_ps = [ps.tile([P, N], F32, name=f"b_ps{t}") for t in range(TILES)]
+
+        def a_bank(i):
+            return ps.tile([P, N], F32, name=f"a_bank{i}")
+
+        def load_x(z):
+            nc.sync.dma_start(x_win[z][:], xt_words[z].rearrange("p n t -> p (n t)").bitcast(I32))
+
+        def load_w(z, h):
+            nc.sync.dma_start(w_raw[z, h][:], wn[512 * z : 512 * (z + 1), HALF * h : HALF * (h + 1)].rearrange("(p t) n -> p t n", t=4))
+
+        def load_g(c):
+            nc.sync.dma_start(g_win[c][:], g[P * c : P * (c + 1), :])
+
+        def load_s():
+            for q in range(4):
+                nc.sync.dma_start(s_win[32 * q : 32 * q + 8, :].bitcast(I32), xt_scales[:, 4 * q : 4 * q + 4, :].bitcast(I32))
+
+        def load_of():
+            nc.sync.dma_start(of_rows[0:4, :], of.rearrange("o (c p) -> (o c) p", p=P))
+
+        def load_rw():
+            nc.gpsimd.dma_start(rw_rows[0:4, :], rw.rearrange("(c p) o -> c (p o)", p=P))
+
+        def turn_rows(rows, col, i):
+            bank = a_bank(i)
+            nc.tensor.transpose(bank[:, 0:P], rows[:], ident[:])
+            nc.scalar.copy(col[:], bank[:, 0:4])
+
+        def cast(z, h, eng):
+            dst = w_bf[z, h][:].rearrange("p (c i) t -> p c t i", i=4)
+            src = w_raw[z, h][:].rearrange("p t (c i) -> p c t i", i=4)
+            if eng == "s":
+                nc.scalar.copy(dst, src)
+            elif eng == "g":
+                nc.gpsimd.tensor_scalar(dst, src, 1.0, 0.0, ALU.mult, ALU.add)
+            else:
+                nc.vector.tensor_copy(dst, src)
+
+        def quant(z, h):
+            nc.vector.quantize_mx(out=w_codes[z, h][:].bitcast(FP8X4), scales=w_scales[z, h][:], in_=w_bf[z, h][:].rearrange("p n t -> p (n t)"))
+
+        def gather_x(z):
+            nc.vector.tensor_copy(x_codes[z][:], x_win[z][:].bitcast(U32).indirect(offsets[:]))
+
+        def gather_s():
+            nc.vector.tensor_copy(x_scales[:], s_win[:].indirect(offsets[:]))
+
+        def gather_g(c):
+            nc.vector.tensor_copy(g_t[c][:], g_win[c][:].indirect(offsets[:]))
+
+        def gather_last(t):
+            nc.vector.tensor_copy(g_last[t][:], g_win[3][:].indirect(offsets[:, OFFS_PER_TILE * t : OFFS_PER_TILE * (t + 1)]))
+
+        def product(c):
+            h, cc = divmod(c, 2)
+            bank = a_bank(c)
+            for z in range(2):
+                nc.tensor.matmul_mx(
+                    out=bank[:],
+                    lhsT=w_codes[z, h][:, P * cc : P * (cc + 1)].bitcast(FP8X4),
+                    lhsT_scale=w_scales[z, h][:, P * cc : P * (cc + 1)],
+                    rhs=x_codes[z][:].bitcast(FP8X4),
+                    rhs_scale=x_scales[4 * z :, :],
+                    start=(z == 0),
+                    stop=(z == 1),
+                )
+            nc.scalar.activation(a_t[c][:], bank[:], ACT.Identity, bias=of_col[:, c : c + 1])
+
+        def fill(t):
+            for c in range(4):
+                nc.tensor.matmul(b_ps[t][:, P * c : P * (c + 1)], of_col[:, c : c + 1].to_broadcast([P, P]), ident[:], start=(c == 0), stop=False, is_transpose=True)
+
+        def turn_g(c, t):
+            src = g_t[c][:, P * t : P * (t + 1)] if c < 3 else g_last[t][:]
+            nc.tensor.matmul(b_ps[t][:, P * c : P * (c + 1)], src, ident[:], start=False, stop=(c == 3), is_transpose=True)
+
+        a_ps = {}
+
+        def turn_a(c, t):
+            if t not in a_ps:
+                a_ps.update({t: a_bank(t)})
+            nc.tensor.transpose(a_ps[t][:, P * c : P * (c + 1)], a_t[c][:, P * t : P * (t + 1)], ident[:])
+
+        def b_out(t):
+            nc.scalar.activation(b_sb[t][:], b_ps[t][:], ACT.Copy, scale=rw_col[:, t : t + 1])
+
+        def square(t):
+            nc.scalar.activation(scaled[t][:], a_ps[t][:], ACT.Square, accum_out=stat["aa", t][:])
+
+        def inverse(t):
+            nc.gpsimd.tensor_scalar(stat["den", t][:], stat["aa", t][:], 0.1 * N, -1.0, ALU.add, ALU.mult)
+            nc.vector.reciprocal(stat["inv", t][:], stat["den", t][:])
+
+        def dot(t):
+            nc.vector.scalar_tensor_tensor(res[t][:], a_ps[t][:], 1.0, b_sb[t][:], ALU.mult, ALU.mult, accum_out=stat["ab", t][:])
+
+        def coef(t):
+            nc.gpsimd.tensor_scalar(stat["coef", t][:], stat["ab", t][:], stat["inv", t][:], 0.0, ALU.mult, ALU.add)
+
+        def finish(t):
+            nc.vector.scalar_tensor_tensor(res[t][:], a_ps[t][:], stat["coef", t][:], b_sb[t][:], ALU.mult, ALU.add)
+            nc.sync.dma_start(out[P * t : P * (t + 1), :], res[t][:])
+
+        nc.vector.memset(s_win[:].bitcast(I32), 0)
+        nc.vector.memset(of_rows[:], 0.0)
+        nc.vector.memset(rw_rows[:], 0.0)
+        make_identity(nc, ident[:])
+        nc.sync.dma_start(offsets[:], offs)
+        load_x(0)
+        load_w(0, 0)
+        load_s()
+        load_of()
+        load_rw()
+        load_w(1, 0)
+        load_x(1)
+        load_w(0, 1)
+        load_w(1, 1)
+        for c in range(4):
+            load_g(c)
+        turn_rows(of_rows, of_col, 2)
+        turn_rows(rw_rows, rw_col, 3)
+        gather_x(0)
+        cast(0, 0, "s")
+        gather_s()
+        cast(1, 0, "s")
+        gather_x(1)
+        quant(0, 0)
+        quant(1, 0)
+        cast(0, 1, "s")
+        cast(1, 1, "v")
+        quant(0, 1)
+        quant(1, 1)
+        for c in range(4):
+            product(c)
+        for t in range(TILES):
+            fill(t)
+        for c in range(3):
+            gather_g(c)
+        for t in range(TILES):
+            gather_last(t)
+        for t in range(TILES):
+            for c in range(4):
+                turn_a(c, t)
+            square(t)
+            for c in range(4):
+                turn_g(c, t)
+            b_out(t)
+            inverse(t)
+        dot(0)
+        for t in range(TILES):
+            if t < TILES - 1:
+                dot(t + 1)
+            coef(t)
+            finish(t)

@@ -33,22 +33,20 @@ def tile_moe_gradient_off_expert_answer_kernel(tc, xt_words, xt_scales, wn, g, o
         x_win = [sb.tile([P, T], I32, name=f"x_win{z}") for z in range(2)]
         s_win = sb.tile([P, T], U8, name="s_win")
         g_win = [sb.tile([P, T], F32, name=f"g_win{c}") for c in range(4)]
-        w_raw = {(z, h): sb.tile([P, 4, HALF], F32, name=f"w_raw{z}{h}") for z in range(2) for h in range(2)}
-        w_bf = {(z, h): sb.tile([P, HALF, 4], BF16, name=f"w_bf{z}{h}", align_bytes=64) for z in range(2) for h in range(2)}
-        w_codes = {(z, h): sb.tile([P, HALF], U32, name=f"w_codes{z}{h}", align_bytes=64) for z in range(2) for h in range(2)}
-        w_scales = {(z, h): sb.tile([P, HALF], U8, name=f"w_scales{z}{h}", align_bytes=64) for z in range(2) for h in range(2)}
+        w_raw = {(z, h): sb.tile([P, 4, HALF], F32, name=f"w_raw{z}{h}", tag=f"raw{z}{h}") for z in range(2) for h in range(2)}
+        w_bf = {(z, h): sb.tile([P, HALF, 4], BF16, name=f"w_bf{z}{h}", tag=f"stage{z}{h * (1 - z)}", align_bytes=64) for h in range(2) for z in range(2)}
+        w_codes = [sb.tile([P, 2, HALF], U32, name=f"w_codes{h}", align_bytes=64) for h in range(2)]
+        w_scales = [sb.tile([P, 2, HALF], U8, name=f"w_scales{h}", align_bytes=64) for h in range(2)]
         x_codes = [sb.tile([P, J], U32, name=f"x_codes{z}", align_bytes=64) for z in range(2)]
         x_scales = sb.tile([P, J], U8, name="x_scales", align_bytes=64)
-        g_t = [sb.tile([P, J], F32, name=f"g_t{c}") for c in range(3)]
-        g_last = [sb.tile([P, P], F32, name=f"g_last{t}") for t in range(TILES)]
-        a_t = [sb.tile([P, J], F32, name=f"a_t{c}") for c in range(4)]
+        g_t = {}
+        a_t = [sb.tile([P, J], F32, name=f"a_t{c}", tag=("raw01" if c == 0 else f"a_t{c}")) for c in range(4)]
         b_sb = [sb.tile([P, N], F32, name=f"b_sb{t}") for t in range(TILES)]
         res = [sb.tile([P, N], F32, name=f"res{t}") for t in range(TILES)]
         scaled = [sb.tile([P, N], F32, name=f"scaled{t}") for t in range(TILES)]
         ident = sb.tile([P, P], F32, name="ident")
-        of_rows = sb.tile([P, P], F32, name="of_rows")
-        rw_rows = sb.tile([P, P], F32, name="rw_rows")
-        of_col = sb.tile([P, 4], F32, name="of_col")
+        rows = sb.tile([P, P], F32, name="rows")
+        of_col = sb.tile([P, 4], F32, name="of_col", tag="late", align_bytes=64)
         rw_col = sb.tile([P, 4], F32, name="rw_col")
         stat = {(nm, t): sb.tile([P, 1], F32, name=f"{nm}{t}") for nm in ("aa", "ab", "den", "inv", "coef") for t in range(TILES)}
 
@@ -57,11 +55,16 @@ def tile_moe_gradient_off_expert_answer_kernel(tc, xt_words, xt_scales, wn, g, o
         def a_bank(i):
             return ps.tile([P, N], F32, name=f"a_bank{i}")
 
-        def load_x(z):
-            nc.sync.dma_start(x_win[z][:], xt_words[z].rearrange("p n t -> p (n t)").bitcast(I32))
+        def load_x(z, cuts=(0, T)):
+            src = xt_words[z].rearrange("p n t -> p (n t)").bitcast(I32)
+            for lo, hi in zip(cuts, cuts[1:]):
+                nc.sync.dma_start(x_win[z][:, lo:hi], src[:, lo:hi])
 
-        def load_w(z, h):
-            nc.sync.dma_start(w_raw[z, h][:], wn[512 * z : 512 * (z + 1), HALF * h : HALF * (h + 1)].rearrange("(p t) n -> p t n", t=4))
+        def load_w(z, h, parts=1):
+            src = wn[512 * z : 512 * (z + 1), HALF * h : HALF * (h + 1)].rearrange("(p t) n -> p t n", t=4)
+            step = 4 // parts
+            for i in range(parts):
+                nc.sync.dma_start(w_raw[z, h][:, step * i : step * (i + 1), :], src[:, step * i : step * (i + 1), :])
 
         def load_g(c):
             nc.sync.dma_start(g_win[c][:], g[P * c : P * (c + 1), :])
@@ -71,15 +74,15 @@ def tile_moe_gradient_off_expert_answer_kernel(tc, xt_words, xt_scales, wn, g, o
                 nc.sync.dma_start(s_win[32 * q : 32 * q + 8, :].bitcast(I32), xt_scales[:, 4 * q : 4 * q + 4, :].bitcast(I32))
 
         def load_of():
-            nc.sync.dma_start(of_rows[0:4, :], of.rearrange("o (c p) -> (o c) p", p=P))
+            nc.sync.dma_start(rows[0:64, :], of.rearrange("o (c p) -> o c p", p=P).to_broadcast([16, 4, P]))
 
         def load_rw():
-            nc.gpsimd.dma_start(rw_rows[0:4, :], rw.rearrange("(c p) o -> c (p o)", p=P))
+            nc.sync.dma_start(rows[64:P, :], rw.rearrange("(c p) o -> o c p", p=P).to_broadcast([16, 4, P]))
 
-        def turn_rows(rows, col, i):
-            bank = a_bank(i)
-            nc.tensor.transpose(bank[:, 0:P], rows[:], ident[:])
-            nc.scalar.copy(col[:], bank[:, 0:4])
+        def turn_rows():
+            nc.tensor.transpose(b_ps[0][:, 0:P], rows[:], ident[:])
+            nc.scalar.copy(of_col[:], b_ps[0][:, 0:4])
+            nc.scalar.copy(rw_col[:], b_ps[0][:, 64:68])
 
         def cast(z, h, eng):
             dst = w_bf[z, h][:].rearrange("p (c i) t -> p c t i", i=4)
@@ -92,7 +95,7 @@ def tile_moe_gradient_off_expert_answer_kernel(tc, xt_words, xt_scales, wn, g, o
                 nc.vector.tensor_copy(dst, src)
 
         def quant(z, h):
-            nc.vector.quantize_mx(out=w_codes[z, h][:].bitcast(FP8X4), scales=w_scales[z, h][:], in_=w_bf[z, h][:].rearrange("p n t -> p (n t)"))
+            nc.vector.quantize_mx(out=w_codes[h][:, z].bitcast(FP8X4), scales=w_scales[h][:, z], in_=w_bf[z, h][:].rearrange("p n t -> p (n t)"))
 
         def gather_x(z):
             nc.vector.tensor_copy(x_codes[z][:], x_win[z][:].bitcast(U32).indirect(offsets[:]))
@@ -100,11 +103,11 @@ def tile_moe_gradient_off_expert_answer_kernel(tc, xt_words, xt_scales, wn, g, o
         def gather_s():
             nc.vector.tensor_copy(x_scales[:], s_win[:].indirect(offsets[:]))
 
-        def gather_g(c):
-            nc.vector.tensor_copy(g_t[c][:], g_win[c][:].indirect(offsets[:]))
-
-        def gather_last(t):
-            nc.vector.tensor_copy(g_last[t][:], g_win[3][:].indirect(offsets[:, OFFS_PER_TILE * t : OFFS_PER_TILE * (t + 1)]))
+        def gather_g(c, lo=0, hi=TILES):
+            if c // 2 not in g_t:
+                g_t.update({c // 2: sb.tile([P, 2, J], F32, name=f"g_t{c // 2}", tag=("stage10", "late")[c // 2], align_bytes=64)})
+            picked = g_win[c][:].indirect(offsets[:, OFFS_PER_TILE * lo : OFFS_PER_TILE * hi])
+            nc.vector.tensor_copy(g_t[c // 2][:, c % 2, P * lo : P * hi], picked)
 
         def product(c):
             h, cc = divmod(c, 2)
@@ -112,8 +115,8 @@ def tile_moe_gradient_off_expert_answer_kernel(tc, xt_words, xt_scales, wn, g, o
             for z in range(2):
                 nc.tensor.matmul_mx(
                     out=bank[:],
-                    lhsT=w_codes[z, h][:, P * cc : P * (cc + 1)].bitcast(FP8X4),
-                    lhsT_scale=w_scales[z, h][:, P * cc : P * (cc + 1)],
+                    lhsT=w_codes[h][:, z, P * cc : P * (cc + 1)].bitcast(FP8X4),
+                    lhsT_scale=w_scales[h][:, z, P * cc : P * (cc + 1)],
                     rhs=x_codes[z][:].bitcast(FP8X4),
                     rhs_scale=x_scales[4 * z :, :],
                     start=(z == 0),
@@ -126,7 +129,7 @@ def tile_moe_gradient_off_expert_answer_kernel(tc, xt_words, xt_scales, wn, g, o
                 nc.tensor.matmul(b_ps[t][:, P * c : P * (c + 1)], of_col[:, c : c + 1].to_broadcast([P, P]), ident[:], start=(c == 0), stop=False, is_transpose=True)
 
         def turn_g(c, t):
-            src = g_t[c][:, P * t : P * (t + 1)] if c < 3 else g_last[t][:]
+            src = g_t[c // 2][:, c % 2, P * t : P * (t + 1)]
             nc.tensor.matmul(b_ps[t][:, P * c : P * (c + 1)], src, ident[:], start=False, stop=(c == 3), is_transpose=True)
 
         a_ps = {}
@@ -157,29 +160,26 @@ def tile_moe_gradient_off_expert_answer_kernel(tc, xt_words, xt_scales, wn, g, o
             nc.sync.dma_start(out[P * t : P * (t + 1), :], res[t][:])
 
         nc.vector.memset(s_win[:].bitcast(I32), 0)
-        nc.vector.memset(of_rows[:], 0.0)
-        nc.vector.memset(rw_rows[:], 0.0)
-        make_identity(nc, ident[:])
         nc.sync.dma_start(offsets[:], offs)
+        make_identity(nc, ident[:])
+        load_of()
         load_x(0)
+        load_rw()
         load_w(0, 0)
         load_s()
-        load_of()
-        load_rw()
         load_w(1, 0)
         load_x(1)
         load_w(0, 1)
         load_w(1, 1)
         for c in range(4):
             load_g(c)
-        turn_rows(of_rows, of_col, 2)
-        turn_rows(rw_rows, rw_col, 3)
+        turn_rows()
         gather_x(0)
         cast(0, 0, "s")
         gather_s()
         cast(1, 0, "s")
-        gather_x(1)
         quant(0, 0)
+        gather_x(1)
         quant(1, 0)
         cast(0, 1, "s")
         cast(1, 1, "v")
@@ -192,11 +192,14 @@ def tile_moe_gradient_off_expert_answer_kernel(tc, xt_words, xt_scales, wn, g, o
         for c in range(3):
             gather_g(c)
         for t in range(TILES):
-            gather_last(t)
+            gather_g(3, t, t + 1)
         for t in range(TILES):
             for c in range(4):
                 turn_a(c, t)
-            square(t)
+        square(0)
+        for t in range(TILES):
+            if t < TILES - 1:
+                square(t + 1)
             for c in range(4):
                 turn_g(c, t)
             b_out(t)

@@ -32,7 +32,7 @@ def tile_moe_gradient_off_expert_answer_kernel(tc, xt_words, xt_scales, wn, g, o
         offsets = lists.tile([P, J // 16], U16, name="offsets")
         x_win = [sb.tile([P, T], I32, name=f"x_win{z}") for z in range(2)]
         s_win = sb.tile([P, T], U8, name="s_win")
-        g_win = [sb.tile([P, T], F32, name=f"g_win{c}") for c in range(4)]
+        g_win = [sb.tile([P, T], F32, name=f"g_win{c}", tag=f"g_win{c}") for c in range(4)]
         w_raw = {(z, h): sb.tile([P, 4, HALF], F32, name=f"w_raw{z}{h}", tag=f"raw{z}{h}") for z in range(2) for h in range(2)}
         w_bf = {(z, h): sb.tile([P, HALF, 4], BF16, name=f"w_bf{z}{h}", tag=f"stage{z}{h * (1 - z)}", align_bytes=64) for h in range(2) for z in range(2)}
         w_codes = [sb.tile([P, 2, HALF], U32, name=f"w_codes{h}", align_bytes=64) for h in range(2)]
@@ -40,15 +40,18 @@ def tile_moe_gradient_off_expert_answer_kernel(tc, xt_words, xt_scales, wn, g, o
         x_codes = [sb.tile([P, J], U32, name=f"x_codes{z}", align_bytes=64) for z in range(2)]
         x_scales = sb.tile([P, J], U8, name="x_scales", align_bytes=64)
         g_t = {}
-        a_t = [sb.tile([P, J], F32, name=f"a_t{c}", tag=("raw01" if c == 0 else f"a_t{c}")) for c in range(4)]
+        a_t = [sb.tile([P, J], F32, name=f"a_t{c}", tag=("raw01", "a_t1", "a_t2", "a_t3")[c]) for c in range(4)]
         b_sb = [sb.tile([P, N], F32, name=f"b_sb{t}") for t in range(TILES)]
         res = [sb.tile([P, N], F32, name=f"res{t}") for t in range(TILES)]
         scaled = [sb.tile([P, N], F32, name=f"scaled{t}") for t in range(TILES)]
         ident = sb.tile([P, P], F32, name="ident")
         rows = sb.tile([P, P], F32, name="rows")
-        of_col = sb.tile([P, 4], F32, name="of_col", tag="late", align_bytes=64)
-        rw_col = sb.tile([P, 4], F32, name="rw_col")
-        stat = {(nm, t): sb.tile([P, 1], F32, name=f"{nm}{t}") for nm in ("aa", "ab", "den", "inv", "coef") for t in range(TILES)}
+        of_col = sb.tile([P, 4], F32, name="of_col")
+        rw_col = [sb.tile([P, 3], F32, name=f"rw_col{i}", tag=f"small{i}") for i in range(2)]
+        den = sb.tile([P, TILES], F32, name="den")
+        inv = sb.tile([P, TILES], F32, name="inv", tag="g_win3")
+        aa = [sb.tile([P, TILES], F32, name="aa0"), sb.tile([P, TILES], F32, name="aa1", tag="small0")]
+        coef = [sb.tile([P, 1], F32, name=f"coef{t}") for t in range(TILES)]
 
         b_ps = [ps.tile([P, N], F32, name=f"b_ps{t}") for t in range(TILES)]
 
@@ -82,11 +85,12 @@ def tile_moe_gradient_off_expert_answer_kernel(tc, xt_words, xt_scales, wn, g, o
         def turn_rows():
             nc.tensor.transpose(b_ps[0][:, 0:P], rows[:], ident[:])
             nc.scalar.copy(of_col[:], b_ps[0][:, 0:4])
-            nc.scalar.copy(rw_col[:], b_ps[0][:, 64:68])
+            nc.scalar.copy(rw_col[0][:, 0:1], b_ps[0][:, 64:65])
+            nc.scalar.copy(rw_col[1][:], b_ps[0][:, 65:68])
 
-        def cast(z, h, eng):
-            dst = w_bf[z, h][:].rearrange("p (c i) t -> p c t i", i=4)
-            src = w_raw[z, h][:].rearrange("p t (c i) -> p c t i", i=4)
+        def cast(z, h, eng, lo=0, hi=HALF):
+            dst = w_bf[z, h][:, lo:hi, :].rearrange("p (c i) t -> p c t i", i=4)
+            src = w_raw[z, h][:, :, lo:hi].rearrange("p t (c i) -> p c t i", i=4)
             if eng == "s":
                 nc.scalar.copy(dst, src)
             elif eng == "g":
@@ -105,7 +109,7 @@ def tile_moe_gradient_off_expert_answer_kernel(tc, xt_words, xt_scales, wn, g, o
 
         def gather_g(c, lo=0, hi=TILES):
             if c // 2 not in g_t:
-                g_t.update({c // 2: sb.tile([P, 2, J], F32, name=f"g_t{c // 2}", tag=("stage10", "late")[c // 2], align_bytes=64)})
+                g_t.update({c // 2: sb.tile([P, 2, J], F32, name=f"g_t{c // 2}", tag=("stage10", "g_t1")[c // 2], align_bytes=64)})
             picked = g_win[c][:].indirect(offsets[:, OFFS_PER_TILE * lo : OFFS_PER_TILE * hi])
             nc.vector.tensor_copy(g_t[c // 2][:, c % 2, P * lo : P * hi], picked)
 
@@ -140,24 +144,21 @@ def tile_moe_gradient_off_expert_answer_kernel(tc, xt_words, xt_scales, wn, g, o
             nc.tensor.transpose(a_ps[t][:, P * c : P * (c + 1)], a_t[c][:, P * t : P * (t + 1)], ident[:])
 
         def b_out(t):
-            nc.scalar.activation(b_sb[t][:], b_ps[t][:], ACT.Copy, scale=rw_col[:, t : t + 1])
+            nc.scalar.activation(b_sb[t][:], b_ps[t][:], ACT.Copy, scale=rw_col[min(t, 1)][:, max(t - 1, 0) : max(t - 1, 0) + 1])
 
         def square(t):
-            nc.scalar.activation(scaled[t][:], a_ps[t][:], ACT.Square, accum_out=stat["aa", t][:])
+            nc.scalar.activation(scaled[t][:], a_ps[t][:], ACT.Square, accum_out=aa[t // 2][:, t : t + 1])
 
-        def inverse(t):
-            nc.gpsimd.tensor_scalar(stat["den", t][:], stat["aa", t][:], 0.1 * N, -1.0, ALU.add, ALU.mult)
-            nc.vector.reciprocal(stat["inv", t][:], stat["den", t][:])
+        def inverse(lo, hi):
+            nc.gpsimd.tensor_scalar(den[:, lo:hi], aa[lo // 2][:, lo:hi], 0.1 * N, -1.0, ALU.add, ALU.mult)
+            nc.vector.reciprocal(inv[:, lo:hi], den[:, lo:hi])
 
         def dot(t):
-            nc.vector.scalar_tensor_tensor(res[t][:], a_ps[t][:], 1.0, b_sb[t][:], ALU.mult, ALU.mult, accum_out=stat["ab", t][:])
+            nc.vector.scalar_tensor_tensor(res[t][:], a_ps[t][:], inv[:, t : t + 1], b_sb[t][:], ALU.mult, ALU.mult, accum_out=coef[t][:])
 
-        def coef(t):
-            nc.gpsimd.tensor_scalar(stat["coef", t][:], stat["ab", t][:], stat["inv", t][:], 0.0, ALU.mult, ALU.add)
-
-        def finish(t):
-            nc.vector.scalar_tensor_tensor(res[t][:], a_ps[t][:], stat["coef", t][:], b_sb[t][:], ALU.mult, ALU.add)
-            nc.sync.dma_start(out[P * t : P * (t + 1), :], res[t][:])
+        def finish(t, lo=0, hi=N, queue=nc.sync):
+            nc.vector.scalar_tensor_tensor(res[t][:, lo:hi], a_ps[t][:, lo:hi], coef[t][:], b_sb[t][:, lo:hi], ALU.mult, ALU.add)
+            queue.dma_start(out[P * t : P * (t + 1), lo:hi], res[t][:, lo:hi])
 
         nc.vector.memset(s_win[:].bitcast(I32), 0)
         nc.sync.dma_start(offsets[:], offs)
@@ -196,17 +197,20 @@ def tile_moe_gradient_off_expert_answer_kernel(tc, xt_words, xt_scales, wn, g, o
         for t in range(TILES):
             for c in range(4):
                 turn_a(c, t)
-        square(0)
         for t in range(TILES):
-            if t < TILES - 1:
-                square(t + 1)
             for c in range(4):
                 turn_g(c, t)
+        square(0)
+        square(1)
+        inverse(0, 2)
+        b_out(0)
+        for t in range(1, TILES):
+            if t < TILES - 1:
+                square(t + 1)
+                inverse(t + 1, t + 2)
             b_out(t)
-            inverse(t)
         dot(0)
         for t in range(TILES):
             if t < TILES - 1:
                 dot(t + 1)
-            coef(t)
             finish(t)

@@ -47,10 +47,10 @@ def tile_moe_gradient_off_expert_answer_kernel(tc, xt_words, xt_scales, wn, g, o
         ident = sb.tile([P, P], F32, name="ident")
         rows = sb.tile([P, P], F32, name="rows")
         of_col = sb.tile([P, 4], F32, name="of_col")
-        rw_col = [sb.tile([P, 3], F32, name=f"rw_col{i}", tag=f"small{i}") for i in range(2)]
+        rw_col = sb.tile([P, 4], F32, name="rw_col")
         den = sb.tile([P, TILES], F32, name="den")
         inv = sb.tile([P, TILES], F32, name="inv", tag="g_win3")
-        aa = [sb.tile([P, TILES], F32, name="aa0"), sb.tile([P, TILES], F32, name="aa1", tag="small0")]
+        aa = sb.tile([P, TILES], F32, name="aa")
         coef = [sb.tile([P, 1], F32, name=f"coef{t}") for t in range(TILES)]
 
         b_ps = [ps.tile([P, N], F32, name=f"b_ps{t}") for t in range(TILES)]
@@ -85,8 +85,7 @@ def tile_moe_gradient_off_expert_answer_kernel(tc, xt_words, xt_scales, wn, g, o
         def turn_rows():
             nc.tensor.transpose(b_ps[0][:, 0:P], rows[:], ident[:])
             nc.scalar.copy(of_col[:], b_ps[0][:, 0:4])
-            nc.scalar.copy(rw_col[0][:, 0:1], b_ps[0][:, 64:65])
-            nc.scalar.copy(rw_col[1][:], b_ps[0][:, 65:68])
+            nc.scalar.copy(rw_col[:], b_ps[0][:, 64:68])
 
         def cast(z, h, eng, lo=0, hi=HALF):
             dst = w_bf[z, h][:, lo:hi, :].rearrange("p (c i) t -> p c t i", i=4)
@@ -144,13 +143,13 @@ def tile_moe_gradient_off_expert_answer_kernel(tc, xt_words, xt_scales, wn, g, o
             nc.tensor.transpose(a_ps[t][:, P * c : P * (c + 1)], a_t[c][:, P * t : P * (t + 1)], ident[:])
 
         def b_out(t):
-            nc.scalar.activation(b_sb[t][:], b_ps[t][:], ACT.Copy, scale=rw_col[min(t, 1)][:, max(t - 1, 0) : max(t - 1, 0) + 1])
+            nc.scalar.activation(b_sb[t][:], b_ps[t][:], ACT.Copy, scale=rw_col[:, t : t + 1])
 
         def square(t):
-            nc.scalar.activation(scaled[t][:], a_ps[t][:], ACT.Square, accum_out=aa[t // 2][:, t : t + 1])
+            nc.scalar.activation(scaled[t][:], a_ps[t][:], ACT.Square, accum_out=aa[:, t : t + 1])
 
         def inverse(lo, hi):
-            nc.gpsimd.tensor_scalar(den[:, lo:hi], aa[lo // 2][:, lo:hi], 0.1 * N, -1.0, ALU.add, ALU.mult)
+            nc.gpsimd.tensor_scalar(den[:, lo:hi], aa[:, lo:hi], 0.1 * N, -1.0, ALU.add, ALU.mult)
             nc.vector.reciprocal(inv[:, lo:hi], den[:, lo:hi])
 
         def dot(t):
@@ -159,6 +158,11 @@ def tile_moe_gradient_off_expert_answer_kernel(tc, xt_words, xt_scales, wn, g, o
         def finish(t, lo=0, hi=N, queue=nc.sync):
             nc.vector.scalar_tensor_tensor(res[t][:, lo:hi], a_ps[t][:, lo:hi], coef[t][:], b_sb[t][:, lo:hi], ALU.mult, ALU.add)
             queue.dma_start(out[P * t : P * (t + 1), lo:hi], res[t][:, lo:hi])
+
+        def finish_aside(t):
+            nc.scalar.activation(scaled[t][:], a_ps[t][:], ACT.Copy, scale=coef[t][:])
+            nc.gpsimd.tensor_tensor(res[t][:], scaled[t][:], b_sb[t][:], ALU.add)
+            nc.sync.dma_start(out[P * t : P * (t + 1), :], res[t][:])
 
         nc.vector.memset(s_win[:].bitcast(I32), 0)
         nc.sync.dma_start(offsets[:], offs)
@@ -200,17 +204,15 @@ def tile_moe_gradient_off_expert_answer_kernel(tc, xt_words, xt_scales, wn, g, o
         for t in range(TILES):
             for c in range(4):
                 turn_g(c, t)
-        square(0)
-        square(1)
-        inverse(0, 2)
-        b_out(0)
-        for t in range(1, TILES):
-            if t < TILES - 1:
-                square(t + 1)
-                inverse(t + 1, t + 2)
+        for t in range(TILES):
+            square(t)
+        inverse(0, TILES)
+        for t in range(TILES):
             b_out(t)
         dot(0)
-        for t in range(TILES):
+        dot(1)
+        for t in range(1, TILES):
             if t < TILES - 1:
                 dot(t + 1)
             finish(t)
+        finish_aside(0)

from contextlib import ExitStack

import concourse.mybir as mybir
from concourse.masks import make_identity

K, N, T, J = 1024, 512, 1024, 512
FLOPS = 2 * K * N * J

F32 = mybir.dt.float32
BF16 = mybir.dt.bfloat16
I32 = mybir.dt.int32
U32 = mybir.dt.uint32
U16 = mybir.dt.uint16
U8 = mybir.dt.uint8
FP8X4 = mybir.dt.float8_e4m3fn_x4
ACT = mybir.ActivationFunctionType
ALU = mybir.AluOpType

P = 128
HALF = N // 2
TILES = J // P
OFFS_PER_TILE = P // 16


def tile_moe_gradient_off_expert_answer_kernel(tc, xt_words, xt_scales, wn, g, of, rw, offs, out):
    nc = tc.nc
    with ExitStack() as ctx:
        lists = ctx.enter_context(tc.tile_pool(name="lists", bufs=1))
        sb = ctx.enter_context(tc.tile_pool(name="sb", bufs=1))
        ps = ctx.enter_context(tc.psum_pool(name="ps", bufs=1))

        offsets = lists.tile([P, J // 16], U16, name="offsets")
        x_win = [sb.tile([P, T], I32, name=f"x_win{z}") for z in range(2)]
        s_win = sb.tile([P, T], U8, name="s_win")
        g_win = [sb.tile([P, T], F32, name=f"g_win{c}", tag=f"g_win{c}") for c in range(4)]
        w_raw = {(z, h): sb.tile([P, 4, HALF], F32, name=f"w_raw{z}{h}", tag=f"raw{z}{h}") for z in range(2) for h in range(2)}
        w_bf = {(z, h): sb.tile([P, HALF, 4], BF16, name=f"w_bf{z}{h}", tag=f"stage{z}{h * (1 - z)}", align_bytes=64) for h in range(2) for z in range(2)}
        w_codes = [sb.tile([P, 2, HALF], U32, name=f"w_codes{h}", align_bytes=64) for h in range(2)]
        w_scales = [sb.tile([P, 2, HALF], U8, name=f"w_scales{h}", align_bytes=64) for h in range(2)]
        x_codes = [sb.tile([P, J], U32, name=f"x_codes{z}", align_bytes=64) for z in range(2)]
        x_scales = sb.tile([P, J], U8, name="x_scales", align_bytes=64)
        g_t = {}
        a_t = [sb.tile([P, J], F32, name=f"a_t{c}", tag=("raw01", "a_t1", "a_t2", "a_t3")[c]) for c in range(4)]
        b_sb = [sb.tile([P, N], F32, name=f"b_sb{t}") for t in range(TILES)]
        res = [sb.tile([P, N], F32, name=f"res{t}") for t in range(TILES)]
        scaled = [sb.tile([P, N], F32, name=f"scaled{t}") for t in range(TILES)]
        ident = sb.tile([P, P], F32, name="ident")
        rows = sb.tile([P, P], F32, name="rows")
        of_col = sb.tile([P, 4], F32, name="of_col")
        rw_col = sb.tile([P, 4], F32, name="rw_col")
        den = sb.tile([P, TILES], F32, name="den")
        inv = sb.tile([P, TILES], F32, name="inv", tag="g_win3")
        aa = sb.tile([P, TILES], F32, name="aa")
        coef = [sb.tile([P, 1], F32, name=f"coef{t}") for t in range(TILES)]

        b_ps = [ps.tile([P, N], F32, name=f"b_ps{t}") for t in range(TILES)]

        def a_bank(i):
            return ps.tile([P, N], F32, name=f"a_bank{i}")

        def load_x(z, cuts=(0, T)):
            src = xt_words[z].rearrange("p n t -> p (n t)").bitcast(I32)
            for lo, hi in zip(cuts, cuts[1:]):
                nc.sync.dma_start(x_win[z][:, lo:hi], src[:, lo:hi])

        def load_w(z, h, parts=1):
            src = wn[512 * z : 512 * (z + 1), HALF * h : HALF * (h + 1)].rearrange("(p t) n -> p t n", t=4)
            step = 4 // parts
            for i in range(parts):
                nc.sync.dma_start(w_raw[z, h][:, step * i : step * (i + 1), :], src[:, step * i : step * (i + 1), :])

        def load_g(c):
            nc.sync.dma_start(g_win[c][:], g[P * c : P * (c + 1), :])

        def load_s():
            for q in range(4):
                nc.sync.dma_start(s_win[32 * q : 32 * q + 8, :].bitcast(I32), xt_scales[:, 4 * q : 4 * q + 4, :].bitcast(I32))

        def load_of():
            nc.sync.dma_start(rows[0:64, :], of.rearrange("o (c p) -> o c p", p=P).to_broadcast([16, 4, P]))

        def load_rw():
            nc.sync.dma_start(rows[64:P, :], rw.rearrange("(c p) o -> o c p", p=P).to_broadcast([16, 4, P]))

        def turn_rows():
            nc.tensor.transpose(b_ps[0][:, 0:P], rows[:], ident[:])
            nc.scalar.copy(of_col[:], b_ps[0][:, 0:4])
            nc.scalar.copy(rw_col[:], b_ps[0][:, 64:68])

        def cast(z, h, eng, lo=0, hi=HALF):
            dst = w_bf[z, h][:, lo:hi, :].rearrange("p (c i) t -> p c t i", i=4)
            src = w_raw[z, h][:, :, lo:hi].rearrange("p t (c i) -> p c t i", i=4)
            if eng == "s":
                nc.scalar.copy(dst, src)
            elif eng == "g":
                nc.gpsimd.tensor_scalar(dst, src, 1.0, 0.0, ALU.mult, ALU.add)
            else:
                nc.vector.tensor_copy(dst, src)

        def quant(z, h):
            nc.vector.quantize_mx(out=w_codes[h][:, z].bitcast(FP8X4), scales=w_scales[h][:, z], in_=w_bf[z, h][:].rearrange("p n t -> p (n t)"))

        def gather_x(z):
            nc.vector.tensor_copy(x_codes[z][:], x_win[z][:].bitcast(U32).indirect(offsets[:]))

        def gather_s():
            nc.vector.tensor_copy(x_scales[:], s_win[:].indirect(offsets[:]))

        def gather_g(c, lo=0, hi=TILES):
            if c // 2 not in g_t:
                g_t.update({c // 2: sb.tile([P, 2, J], F32, name=f"g_t{c // 2}", tag=("stage10", "g_t1")[c // 2], align_bytes=64)})
            picked = g_win[c][:].indirect(offsets[:, OFFS_PER_TILE * lo : OFFS_PER_TILE * hi])
            nc.vector.tensor_copy(g_t[c // 2][:, c % 2, P * lo : P * hi], picked)

        def product(c):
            h, cc = divmod(c, 2)
            bank = a_bank(c)
            for z in range(2):
                nc.tensor.matmul_mx(
                    out=bank[:],
                    lhsT=w_codes[h][:, z, P * cc : P * (cc + 1)].bitcast(FP8X4),
                    lhsT_scale=w_scales[h][:, z, P * cc : P * (cc + 1)],
                    rhs=x_codes[z][:].bitcast(FP8X4),
                    rhs_scale=x_scales[4 * z :, :],
                    start=(z == 0),
                    stop=(z == 1),
                )
            nc.scalar.activation(a_t[c][:], bank[:], ACT.Identity, bias=of_col[:, c : c + 1])

        def fill(t):
            for c in range(4):
                nc.tensor.matmul(b_ps[t][:, P * c : P * (c + 1)], of_col[:, c : c + 1].to_broadcast([P, P]), ident[:], start=(c == 0), stop=False, is_transpose=True)

        def turn_g(c, t):
            src = g_t[c // 2][:, c % 2, P * t : P * (t + 1)]
            nc.tensor.matmul(b_ps[t][:, P * c : P * (c + 1)], src, ident[:], start=False, stop=(c == 3), is_transpose=True)

        a_ps = {}

        def turn_a(c, t):
            if t not in a_ps:
                a_ps.update({t: a_bank(t)})
            nc.tensor.transpose(a_ps[t][:, P * c : P * (c + 1)], a_t[c][:, P * t : P * (t + 1)], ident[:])

        def b_out(t):
            nc.scalar.activation(b_sb[t][:], b_ps[t][:], ACT.Copy, scale=rw_col[:, t : t + 1])

        def square(t):
            nc.scalar.activation(scaled[t][:], a_ps[t][:], ACT.Square, accum_out=aa[:, t : t + 1])

        def inverse(lo, hi):
            nc.gpsimd.tensor_scalar(den[:, lo:hi], aa[:, lo:hi], 0.1 * N, -1.0, ALU.add, ALU.mult)
            nc.vector.reciprocal(inv[:, lo:hi], den[:, lo:hi])

        def dot(t):
            nc.vector.scalar_tensor_tensor(res[t][:], a_ps[t][:], inv[:, t : t + 1], b_sb[t][:], ALU.mult, ALU.mult, accum_out=coef[t][:])

        def finish(t, lo=0, hi=N, queue=nc.sync):
            nc.vector.scalar_tensor_tensor(res[t][:, lo:hi], a_ps[t][:, lo:hi], coef[t][:], b_sb[t][:, lo:hi], ALU.mult, ALU.add)
            queue.dma_start(out[P * t : P * (t + 1), lo:hi], res[t][:, lo:hi])

        def finish_aside(t):
            nc.scalar.activation(scaled[t][:], a_ps[t][:], ACT.Copy, scale=coef[t][:])
            nc.gpsimd.tensor_tensor(res[t][:], scaled[t][:], b_sb[t][:], ALU.add)
            nc.sync.dma_start(out[P * t : P * (t + 1), :], res[t][:])

        nc.vector.memset(s_win[:].bitcast(I32), 0)
        nc.sync.dma_start(offsets[:], offs)
        make_identity(nc, ident[:])
        load_of()
        load_x(0)
        load_rw()
        load_w(0, 0)
        load_s()
        load_w(1, 0)
        load_x(1)
        load_w(0, 1)
        load_w(1, 1)
        for c in range(4):
            load_g(c)
        turn_rows()
        gather_x(0)
        cast(0, 0, "s")
        gather_s()
        cast(1, 0, "s")
        quant(0, 0)
        gather_x(1)
        quant(1, 0)
        cast(0, 1, "s")
        cast(1, 1, "v")
        quant(0, 1)
        quant(1, 1)
        for c in range(4):
            product(c)
        for t in range(TILES):
            fill(t)
        for c in range(3):
            gather_g(c)
        for t in range(TILES):
            gather_g(3, t, t + 1)
        for t in range(TILES):
            for c in range(4):
                turn_a(c, t)
        for t in range(TILES):
            for c in range(4):
                turn_g(c, t)
        for t in range(TILES):
            square(t)
        inverse(0, TILES)
        for t in range(TILES):
            b_out(t)
        dot(0)
        dot(1)
        for t in range(1, TILES):
            if t < TILES - 1:
                dot(t + 1)
            finish(t)
        finish_aside(0)
